import numpy as np
import ml_dtypes


def mxq(x, axis, fmt="e4m3"):
    dtype, down = {"e4m3": (ml_dtypes.float8_e4m3fn, 7), "e5m2": (ml_dtypes.float8_e5m2, 14)}[fmt]
    v = np.moveaxis(np.asarray(x, np.float32).astype(ml_dtypes.bfloat16).astype(np.float64), axis, -1)
    blocks = v.reshape(v.shape[:-1] + (-1, 32))
    amax = np.abs(blocks).max(-1, keepdims=True)
    byte = np.maximum(np.where(amax > 0, np.frexp(amax)[1] - 1 + 127, 0) - down, 1)
    scale = np.exp2(byte - 127.0)
    codes = (blocks / scale).astype(np.float32).astype(dtype).astype(np.float64)
    return np.moveaxis((codes * scale).reshape(v.shape), -1, axis)


WIDE = False


def mx_kscale(k):
    if not WIDE:
        return np.ones(k)
    levels = np.array([10, -10, 5, -5, 0])
    if k % 512:
        return np.exp2(np.random.permutation(np.resize(levels, k // 32))).repeat(32)
    a = np.empty((k // 512, 16))
    for p in range(k // 512):
        a[p, :8] = np.random.permutation(np.resize(levels, 8))
        for g in range(8):
            far = levels[np.abs(levels - a[p, g]) >= 10]
            a[p, g + 8] = far[np.random.randint(len(far))]
    return np.exp2(a.ravel()).repeat(32)


def f64(x):
    return np.asarray(x).astype(np.float64)


def striped(idx):
    return np.tile(idx.reshape(-1, 16).T, (8, 1)).astype(np.uint16)


def unstriped(offs):
    return offs[:16].T.reshape(-1).astype(np.int64)


def striped8(idx):
    return np.concatenate([x.reshape(-1, 16).T for x in idx]).astype(np.uint16)


def runs(offs, k):
    lists = np.stack([offs[16 * r : 16 * r + 16].T.reshape(-1) for r in range(8)]).astype(np.int64)
    return lists[np.arange(k) % 512 // 64]


def pack_weight(w):
    k, n = w.shape
    w = f64(np.asarray(w, np.float32).astype(ml_dtypes.bfloat16)).reshape(k // 32, 32, n)
    amax = np.abs(w).max(1)
    byte = np.clip(np.where(amax > 0, np.frexp(amax)[1] - 1 + 127 - 7, 1), 1, 254)
    scaled = (w * np.exp2(127.0 - byte)[:, None, :]).reshape(k, n).astype(np.float32)
    words = np.ascontiguousarray(scaled.reshape(k // 512, 128, 4, n).transpose(0, 1, 3, 2)).astype(ml_dtypes.float8_e4m3fn).view(np.uint8)
    return words, np.ascontiguousarray(byte.astype(np.uint8).reshape(k // 512, 16, n))


def unpack_weight(words, scales):
    g, p, n, _ = words.shape
    vals = np.ascontiguousarray(words).view(ml_dtypes.float8_e4m3fn).astype(np.float64) * np.repeat(np.exp2(scales.astype(np.float64) - 127.0), 8, axis=1)[..., None]
    return vals.transpose(0, 1, 3, 2).reshape(g * 512, n)


def sigmoid(v):
    return 1.0 / (1.0 + np.exp(-np.maximum(v, -700.0)))


K, T, S, H, G = 512, 1024, 256, 512, 2048


def setup_inputs():
    n = np.random.standard_normal
    s = mx_kscale(K)[:, None]
    packed_xT = pack_weight(n((K, T)) * s)
    packed_w1 = pack_weight(n((K, H)) / np.sqrt(2 * K) / s)
    packed_w2 = pack_weight(n((K, H)) / np.sqrt(2 * K) / s)
    packed_dT = pack_weight(n((K, G)) / s)
    return {
        "x_words": packed_xT[0],
        "x_scales": packed_xT[1],
        "w1_words": packed_w1[0],
        "w1_scales": packed_w1[1],
        "w2_words": packed_w2[0],
        "w2_scales": packed_w2[1],
        "gs": (np.random.uniform(0.5, 1.5, (K, 1)) * s).astype(np.float32),
        "d_words": packed_dT[0],
        "d_scales": packed_dT[1],
        "sl": np.random.uniform(1.0, 2.0, (H, 1)).astype(np.float32),
        "th": (0.5 * n((H, 1))).astype(np.float32),
        "offs": striped8(np.random.randint(0, T, (8, S))),
        "hz": striped8(np.random.randint(0, T, (8, S))),
        "k1": striped8(np.random.randint(0, G, (8, H))),
        "n1": striped(np.random.permutation(S)),
        "n2": striped(np.random.permutation(S)),
    }


def reference(x_words, x_scales, w1_words, w1_scales, w2_words, w2_scales, gs, d_words, d_scales, sl, th, offs, hz, k1, n1, n2):
    d_k1 = unpack_weight(d_words, d_scales)[np.arange(K)[:, None], runs(k1, K)]
    xq = unpack_weight(x_words, x_scales)[np.arange(K)[:, None], runs(offs, K)]
    x_hz = unpack_weight(x_words, x_scales)[np.arange(K)[:, None], runs(hz, K)]
    y = unpack_weight(w1_words, w1_scales).T @ xq + unpack_weight(w2_words, w2_scales).T @ x_hz
    z = f64(gs) * y
    h = 0.0625 * ((d_k1.T @ mxq(z, 0, "e4m3")))
    ds = np.zeros((H, S))
    ds[:, unstriped(n1)] = h
    sg = sigmoid(f64(sl) * (ds[:, unstriped(n2)] - f64(th)))
    return h * sg

@@ -1,0 +1,214 @@
+from contextlib import ExitStack
+
+import concourse.mybir as mybir
+
+K, T, S, H, G = 512, 1024, 256, 512, 2048
+FLOPS = 3 * 2 * K * H * S
+
+F32 = mybir.dt.float32
+BF16 = mybir.dt.bfloat16
+I32 = mybir.dt.int32
+U32 = mybir.dt.uint32
+U16 = mybir.dt.uint16
+U8 = mybir.dt.uint8
+FP8X4 = mybir.dt.float8_e4m3fn_x4
+ACT = mybir.ActivationFunctionType
+ALU = mybir.AluOpType
+
+P = 128
+PACK = 4
+HALF = 128
+COLS = 16
+
+
+def tile_picked_dhqierl_none_p_kernel(
+    tc, x_words, x_scales, w1_words, w1_scales, w2_words, w2_scales, gs, d_words, d_scales, sl, th, offs, hz, k1, n1, n2, out
+):
+    nc = tc.nc
+    with ExitStack() as ctx:
+        keep = ctx.enter_context(tc.tile_pool(name="keep", bufs=1))
+        psum = ctx.enter_context(tc.psum_pool(name="psum", bufs=1))
+
+        def tile(shape, dtype, name, tag=None):
+            return keep.tile(shape, dtype, name=name, tag=tag or name, align_bytes=64)
+
+        def load_list(src, name):
+            dst = keep.tile([P, src.shape[1]], U16, name=name)
+            nc.sync.dma_start(dst[:], src)
+            return dst
+
+        def load_words(queue, src, name):
+            dst = tile([P, src.shape[2]], U32, name)
+            queue.dma_start(out=dst[:].bitcast(I32), in_=src[0].rearrange("p n t -> p (n t)").bitcast(I32))
+            return dst
+
+        def zeroed(width, name, tag=None):
+            dst = tile([P, width], U8, name, tag)
+            nc.vector.memset(dst[:].bitcast(I32), 0)
+            return dst
+
+        def load_scales(queue, dst, src):
+            queue.dma_start(out=dst.bitcast(I32), in_=src[0].bitcast(I32))
+
+        def place_rows(plane):
+            for j in range(1, PACK):
+                nc.sync.dma_start(out=plane[j:P:32, :].bitcast(I32), in_=plane[8 * j : P : 32, :].bitcast(I32))
+
+        def half_of(lst, b):
+            return lst[:, b * HALF // COLS : (b + 1) * HALF // COLS]
+
+        xs_tab = zeroed(T, "xs_tab")
+        ws_raw = zeroed(2 * H, "ws_raw", "slot_a")
+        ds_tab = zeroed(G, "ds_tab")
+        warm_in = tile([P, 1], F32, "warm_in")
+        nc.vector.memset(warm_in[:], 0.0)
+        warm_out = tile([P, 1], F32, "warm_out")
+        nc.scalar.activation(out=warm_out[:], in_=warm_in[:], func=ACT.Sigmoid)
+
+        offs_t = load_list(offs, "offs_t")
+        xw_tab = load_words(nc.scalar, x_words, "xw_tab")
+        load_scales(nc.sync, xs_tab[0:P:8, :], x_scales)
+        load_scales(nc.scalar, ws_raw[0:P:8, 0:H], w1_scales)
+        k1_t = load_list(k1, "k1_t")
+        load_scales(nc.scalar, ws_raw[0:P:8, H : 2 * H], w2_scales)
+        hz_t = load_list(hz, "hz_t")
+        w1_raw = load_words(nc.scalar, w1_words, "w1_raw")
+        w2_raw = load_words(nc.sync, w2_words, "w2_raw")
+        load_scales(nc.scalar, ds_tab[0:P:8, :], d_scales)
+        n1_t = load_list(n1, "n1_t")
+        dw_tab = load_words(nc.scalar, d_words, "dw_tab")
+        n2_t = load_list(n2, "n2_t")
+
+        gs_t = tile([P, PACK], F32, "gs_t")
+        nc.gpsimd.dma_start(out=gs_t[:], in_=gs.rearrange("(p t) o -> p (t o)", t=PACK))
+        sl_t = tile([P, PACK], F32, "sl_t")
+        th_t = tile([P, PACK], F32, "th_t")
+        with nc.allow_non_contiguous_dma(reason="one value a row, rows on the partitions"):
+            nc.gpsimd.dma_start(out=sl_t[:], in_=sl.rearrange("(t p) o -> p (t o)", p=P))
+            nc.gpsimd.dma_start(out=th_t[:], in_=th.rearrange("(t p) o -> p (t o)", p=P))
+        neg_sl = tile([P, PACK], F32, "neg_sl")
+        nc.gpsimd.tensor_scalar(neg_sl[:], sl_t[:], -1.0, 0.0, ALU.mult, ALU.add)
+        bias_t = tile([P, PACK], F32, "bias_t")
+        nc.gpsimd.tensor_tensor(bias_t[:], neg_sl[:], th_t[:], ALU.mult)
+
+        x_lists = (offs_t, hz_t)
+
+        plane_a = tile([P, 2 * HALF + 2 * H], U8, "plane_a")
+        got_a = tile([P, 2 * HALF], U8, "got_a", "slot_b")
+        nc.vector.tensor_copy(got_a[:, 0:HALF], xs_tab[:].indirect(half_of(offs_t, 0)))
+        nc.vector.tensor_copy(
+            out=plane_a[:, 2 * HALF :].rearrange("p (a t m) -> p a t m", a=2, t=PACK),
+            in_=ws_raw[:].rearrange("p (a m t) -> p a t m", a=2, t=PACK),
+        )
+        nc.vector.tensor_copy(got_a[:, HALF : 2 * HALF], xs_tab[:].indirect(half_of(hz_t, 0)))
+        nc.vector.tensor_copy(out=plane_a[:, 0 : 2 * HALF].bitcast(I32), in_=got_a[:].bitcast(I32))
+        place_rows(plane_a)
+
+        w_dealt = []
+        for a, raw in enumerate((w1_raw, w2_raw)):
+            dealt = tile([P, H], U32, "w_dealt%d" % a)
+            nc.scalar.copy(out=dealt[:].rearrange("p (t m) -> p m t", t=PACK), in_=raw[:].rearrange("p (m t) -> p m t", t=PACK))
+            w_dealt.append(dealt)
+
+        def pick_words(b, tag):
+            got = tile([P, 2 * HALF], U32, "xw_got%d" % b, tag)
+            for a in range(2):
+                nc.vector.tensor_copy(got[:, a * HALF : (a + 1) * HALF], xw_tab[:].indirect(half_of(x_lists[a], b)))
+            return got
+
+        def first_product(b, got, plane):
+            acc = psum.tile([P, PACK, HALF], F32, name="y_ps%d" % b)
+            for t in range(PACK):
+                for a in range(2):
+                    c0 = 2 * HALF + a * H + t * P
+                    nc.tensor.matmul_mx(
+                        out=acc[:, t, :],
+                        lhsT=w_dealt[a][:, t * P : (t + 1) * P].bitcast(FP8X4),
+                        lhsT_scale=plane_a[:, c0 : c0 + P],
+                        rhs=got[:, a * HALF : (a + 1) * HALF].bitcast(FP8X4),
+                        rhs_scale=plane[:, a * HALF : (a + 1) * HALF],
+                        start=(a == 0),
+                        stop=(a == 1),
+                    )
+            return acc
+
+        xw_got0 = pick_words(0, "slot_a")
+        y_ps0 = first_product(0, xw_got0, plane_a)
+
+        plane_b = tile([P, 2 * HALF + H], U8, "plane_b")
+        got_b = tile([P, 2 * HALF + H], U8, "got_b", "slot_b")
+        for a in range(2):
+            nc.vector.tensor_copy(got_b[:, a * HALF : (a + 1) * HALF], xs_tab[:].indirect(half_of(x_lists[a], 1)))
+        nc.vector.tensor_copy(got_b[:, 2 * HALF :], ds_tab[:].indirect(k1_t[:]))
+        nc.vector.tensor_copy(out=plane_b[:].bitcast(I32), in_=got_b[:].bitcast(I32))
+        place_rows(plane_b)
+
+        xw_got1 = pick_words(1, "slot_b")
+        y_ps1 = first_product(1, xw_got1, plane_b)
+
+        h_sb = [tile([P, S], F32, "h_sb%d" % t) for t in range(PACK)]
+        ds_sb = [tile([P, S], F32, "ds_sb%d" % t) for t in range(PACK)]
+
+        def weigh(b, acc, tag):
+            z_bf = tile([P, HALF, PACK], BF16, "z_bf%d" % b, tag)
+            nc.vector.tensor_tensor(
+                z_bf[:], acc[:].rearrange("p t n -> p n t"), gs_t[:].unsqueeze(1).to_broadcast([P, HALF, PACK]), ALU.mult
+            )
+            return z_bf
+
+        def quantise(b, z_bf):
+            codes = tile([P, HALF], U32, "z_codes%d" % b)
+            scales = tile([P, HALF], U8, "z_scales%d" % b)
+            nc.vector.quantize_mx(out=codes[:].bitcast(FP8X4), scales=scales[:], in_=z_bf[:].rearrange("p n t -> p (n t)"))
+            return codes, scales
+
+        def pick_dictionary(u, tag):
+            got = tile([P, 2 * P], U32, "dw_got%d" % u, tag)
+            nc.vector.tensor_copy(got[:], dw_tab[:].indirect(k1_t[:, 16 * u : 16 * (u + 1)]))
+            return got
+
+        def second_product(b, ts, got, z):
+            bank = psum.tile([P, len(ts), HALF], F32, name="h_ps%d%d" % (b, ts[0]))
+            for v, t in enumerate(ts):
+                c0 = 2 * HALF + t * P
+                nc.tensor.matmul_mx(
+                    out=bank[:, v, :],
+                    lhsT=got[:, (t % 2) * P : (t % 2 + 1) * P].bitcast(FP8X4),
+                    lhsT_scale=plane_b[:, c0 : c0 + P],
+                    rhs=z[0][:].bitcast(FP8X4),
+                    rhs_scale=z[1][:],
+                    start=True,
+                    stop=True,
+                )
+            for v, t in enumerate(ts):
+                h_part = h_sb[t][:, b * HALF : (b + 1) * HALF]
+                if b == 0 and t == 0:
+                    nc.scalar.activation(out=h_part, in_=bank[:, v, :], func=ACT.Copy, scale=0.0625)
+                else:
+                    nc.vector.tensor_scalar(h_part, bank[:, v, :], 0.0625, None, ALU.mult)
+                nc.scalar.activation(out=ds_sb[t][:].indirect(half_of(n1_t, b)), in_=h_part, func=ACT.Copy)
+
+        z_bf0 = weigh(0, y_ps0, "slot_c")
+        dw_got0 = pick_dictionary(0, "slot_a")
+        z0 = quantise(0, z_bf0)
+        second_product(0, [0], dw_got0, z0)
+        second_product(0, [1], dw_got0, z0)
+        dw_got1 = pick_dictionary(1, "slot_c")
+        second_product(0, [2, 3], dw_got1, z0)
+        z1 = quantise(1, weigh(1, y_ps1, None))
+        second_product(1, [0, 1], dw_got0, z1)
+        second_product(1, [2, 3], dw_got1, z1)
+
+        for t in range(PACK):
+            sg = tile([P, S], F32, "sg%d" % t)
+            for b in range(2):
+                nc.scalar.activation(
+                    out=sg[:, b * HALF : (b + 1) * HALF],
+                    in_=ds_sb[t][:].indirect(half_of(n2_t, b)),
+                    func=ACT.Sigmoid,
+                    scale=sl_t[:, t : t + 1],
+                    bias=bias_t[:, t : t + 1],
+                )
+            res = tile([P, S], F32, "res%d" % t)
+            nc.vector.tensor_tensor(res[:], h_sb[t][:], sg[:], ALU.mult)
+            nc.sync.dma_start(out=out[t * P : (t + 1) * P, :], in_=res[:])

@@ -27,9 +27,12 @@ def tile_picked_dhqierl_none_p_kernel(
     nc = tc.nc
     with ExitStack() as ctx:
         keep = ctx.enter_context(tc.tile_pool(name="keep", bufs=1))
+        stage = ctx.enter_context(tc.tile_pool(name="stage", bufs=1))
         psum = ctx.enter_context(tc.psum_pool(name="psum", bufs=1))
 
         def tile(shape, dtype, name, tag=None):
+            if isinstance(tag, int):
+                return stage.tile(shape, dtype, name=name, offset=tag, align_bytes=64)
             return keep.tile(shape, dtype, name=name, tag=tag or name, align_bytes=64)
 
         def load_list(src, name):
@@ -37,18 +40,17 @@ def tile_picked_dhqierl_none_p_kernel(
             nc.sync.dma_start(dst[:], src)
             return dst
 
-        def load_words(queue, src, name):
-            dst = tile([P, src.shape[2]], U32, name)
+        def load_words(queue, src, name, tag=None):
+            dst = tile([P, src.shape[2]], U32, name, tag)
             queue.dma_start(out=dst[:].bitcast(I32), in_=src[0].rearrange("p n t -> p (n t)").bitcast(I32))
-            return dst
-
-        def zeroed(width, name, tag=None):
-            dst = tile([P, width], U8, name, tag)
-            nc.vector.memset(dst[:].bitcast(I32), 0)
             return dst
 
         def load_scales(queue, dst, src):
             queue.dma_start(out=dst.bitcast(I32), in_=src[0].bitcast(I32))
+
+        def load_repeated(queue, dst, src):
+            rows = src[0].bitcast(I32)
+            queue.dma_start(out=dst.bitcast(I32), in_=rows.unsqueeze(1).to_broadcast([16, 8, rows.shape[1]]))
 
         def place_rows(plane):
             for j in range(1, PACK):
@@ -57,58 +59,55 @@ def tile_picked_dhqierl_none_p_kernel(
         def half_of(lst, b):
             return lst[:, b * HALF // COLS : (b + 1) * HALF // COLS]
 
-        xs_tab = zeroed(T, "xs_tab")
-        ws_raw = zeroed(2 * H, "ws_raw", "slot_a")
-        ds_tab = zeroed(G, "ds_tab")
+        xs_tab = tile([P, T], U8, "xs_tab")
+        ds_tab = tile([P, G], U8, "ds_tab")
+        nc.vector.memset(ds_tab[:].bitcast(I32), 0)
+        w1s_raw = tile([P, H], U8, "w1s_raw")
+        w2s_raw = tile([P, H], U8, "w2s_raw")
+        offs_t = load_list(offs, "offs_t")
+        load_repeated(nc.scalar, w1s_raw[:], w1_scales)
+        load_repeated(nc.sync, xs_tab[:], x_scales)
+        load_repeated(nc.scalar, w2s_raw[:], w2_scales)
+        hz_t = load_list(hz, "hz_t")
+        xw_tab = load_words(nc.scalar, x_words, "xw_tab")
+        k1_t = load_list(k1, "k1_t")
+        w1_raw = load_words(nc.scalar, w1_words, "w1_raw")
         warm_in = tile([P, 1], F32, "warm_in")
         nc.vector.memset(warm_in[:], 0.0)
         warm_out = tile([P, 1], F32, "warm_out")
         nc.scalar.activation(out=warm_out[:], in_=warm_in[:], func=ACT.Sigmoid)
 
-        offs_t = load_list(offs, "offs_t")
-        xw_tab = load_words(nc.scalar, x_words, "xw_tab")
-        load_scales(nc.sync, xs_tab[0:P:8, :], x_scales)
-        load_scales(nc.scalar, ws_raw[0:P:8, 0:H], w1_scales)
-        k1_t = load_list(k1, "k1_t")
-        load_scales(nc.scalar, ws_raw[0:P:8, H : 2 * H], w2_scales)
-        hz_t = load_list(hz, "hz_t")
-        w1_raw = load_words(nc.scalar, w1_words, "w1_raw")
-        w2_raw = load_words(nc.sync, w2_words, "w2_raw")
-        load_scales(nc.scalar, ds_tab[0:P:8, :], d_scales)
-        n1_t = load_list(n1, "n1_t")
-        dw_tab = load_words(nc.scalar, d_words, "dw_tab")
-        n2_t = load_list(n2, "n2_t")
 
+        w2_raw = load_words(nc.sync, w2_words, "w2_raw")
+        load_scales(nc.sync, ds_tab[0:P:8, :], d_scales)
+        n1_t = load_list(n1, "n1_t")
+        n2_t = load_list(n2, "n2_t")
         gs_t = tile([P, PACK], F32, "gs_t")
         nc.gpsimd.dma_start(out=gs_t[:], in_=gs.rearrange("(p t) o -> p (t o)", t=PACK))
-        sl_t = tile([P, PACK], F32, "sl_t")
-        th_t = tile([P, PACK], F32, "th_t")
-        with nc.allow_non_contiguous_dma(reason="one value a row, rows on the partitions"):
-            nc.gpsimd.dma_start(out=sl_t[:], in_=sl.rearrange("(t p) o -> p (t o)", p=P))
-            nc.gpsimd.dma_start(out=th_t[:], in_=th.rearrange("(t p) o -> p (t o)", p=P))
-        neg_sl = tile([P, PACK], F32, "neg_sl")
-        nc.gpsimd.tensor_scalar(neg_sl[:], sl_t[:], -1.0, 0.0, ALU.mult, ALU.add)
-        bias_t = tile([P, PACK], F32, "bias_t")
-        nc.gpsimd.tensor_tensor(bias_t[:], neg_sl[:], th_t[:], ALU.mult)
 
         x_lists = (offs_t, hz_t)
 
         plane_a = tile([P, 2 * HALF + 2 * H], U8, "plane_a")
-        got_a = tile([P, 2 * HALF], U8, "got_a", "slot_b")
-        nc.vector.tensor_copy(got_a[:, 0:HALF], xs_tab[:].indirect(half_of(offs_t, 0)))
-        nc.vector.tensor_copy(
-            out=plane_a[:, 2 * HALF :].rearrange("p (a t m) -> p a t m", a=2, t=PACK),
-            in_=ws_raw[:].rearrange("p (a m t) -> p a t m", a=2, t=PACK),
-        )
-        nc.vector.tensor_copy(got_a[:, HALF : 2 * HALF], xs_tab[:].indirect(half_of(hz_t, 0)))
-        nc.vector.tensor_copy(out=plane_a[:, 0 : 2 * HALF].bitcast(I32), in_=got_a[:].bitcast(I32))
+        for a, raw in enumerate((w1s_raw, w2s_raw)):
+            nc.vector.tensor_copy(
+                out=plane_a[:, 2 * HALF + a * H : 2 * HALF + (a + 1) * H].rearrange("p (t m) -> p t m", t=PACK),
+                in_=raw[:].rearrange("p (m t) -> p t m", t=PACK),
+            )
+        got_a = tile([P, 2112], U8, "got_a", 0)
+        for a in range(2):
+            nc.vector.tensor_copy(got_a[:, a * HALF : (a + 1) * HALF], xs_tab[:].indirect(half_of(x_lists[a], 0)))
+        nc.vector.tensor_copy(out=plane_a[:, 0 : 2 * HALF].bitcast(I32), in_=got_a[:, 0 : 2 * HALF].bitcast(I32))
         place_rows(plane_a)
+        dw_tab = load_words(nc.sync, d_words, "dw_tab", 2048)
 
         w_dealt = []
         for a, raw in enumerate((w1_raw, w2_raw)):
             dealt = tile([P, H], U32, "w_dealt%d" % a)
             nc.scalar.copy(out=dealt[:].rearrange("p (t m) -> p m t", t=PACK), in_=raw[:].rearrange("p (m t) -> p m t", t=PACK))
             w_dealt.append(dealt)
+
+        sl_t = tile([P, PACK], F32, "sl_t", "w1_raw")
+        th_t = tile([P, PACK], F32, "th_t", "w2_raw")
 
         def pick_words(b, tag):
             got = tile([P, 2 * HALF], U32, "xw_got%d" % b, tag)
@@ -117,7 +116,7 @@ def tile_picked_dhqierl_none_p_kernel(
             return got
 
         def first_product(b, got, plane):
-            acc = psum.tile([P, PACK, HALF], F32, name="y_ps%d" % b)
+            acc = psum.tile([P, PACK, HALF], F32, name="y_ps%d" % b, tag=("bank_a", "bank_b")[b])
             for t in range(PACK):
                 for a in range(2):
                     c0 = 2 * HALF + a * H + t * P
@@ -132,34 +131,42 @@ def tile_picked_dhqierl_none_p_kernel(
                     )
             return acc
 
-        xw_got0 = pick_words(0, "slot_a")
+        xw_got0 = pick_words(0, 0)
         y_ps0 = first_product(0, xw_got0, plane_a)
 
         plane_b = tile([P, 2 * HALF + H], U8, "plane_b")
-        got_b = tile([P, 2 * HALF + H], U8, "got_b", "slot_b")
+        got_b = tile([P, 2 * HALF + H], U8, "got_b", 1024)
         for a in range(2):
             nc.vector.tensor_copy(got_b[:, a * HALF : (a + 1) * HALF], xs_tab[:].indirect(half_of(x_lists[a], 1)))
         nc.vector.tensor_copy(got_b[:, 2 * HALF :], ds_tab[:].indirect(k1_t[:]))
         nc.vector.tensor_copy(out=plane_b[:].bitcast(I32), in_=got_b[:].bitcast(I32))
         place_rows(plane_b)
 
-        xw_got1 = pick_words(1, "slot_b")
-        y_ps1 = first_product(1, xw_got1, plane_b)
+        with nc.allow_non_contiguous_dma(reason="one value a row, rows on the partitions"):
+            nc.sync.dma_start(out=sl_t[:], in_=sl.rearrange("(t p) o -> p (t o)", p=P))
+            nc.sync.dma_start(out=th_t[:], in_=th.rearrange("(t p) o -> p (t o)", p=P))
+
+        xw_got1 = pick_words(1, 1024)
 
         h_sb = [tile([P, S], F32, "h_sb%d" % t) for t in range(PACK)]
-        ds_sb = [tile([P, S], F32, "ds_sb%d" % t) for t in range(PACK)]
+        ds_sb = [tile([P, 2 * S], F32, "ds_sb%d" % t) for t in range(PACK)]
 
-        def weigh(b, acc, tag):
+        def quantise(b, acc, tag):
             z_bf = tile([P, HALF, PACK], BF16, "z_bf%d" % b, tag)
-            nc.vector.tensor_tensor(
-                z_bf[:], acc[:].rearrange("p t n -> p n t"), gs_t[:].unsqueeze(1).to_broadcast([P, HALF, PACK]), ALU.mult
-            )
-            return z_bf
-
-        def quantise(b, z_bf):
             codes = tile([P, HALF], U32, "z_codes%d" % b)
             scales = tile([P, HALF], U8, "z_scales%d" % b)
-            nc.vector.quantize_mx(out=codes[:].bitcast(FP8X4), scales=scales[:], in_=z_bf[:].rearrange("p n t -> p (n t)"))
+            pieces = (slice(0, HALF // 2), slice(HALF // 2, HALF))
+            for cols in pieces:
+                nc.vector.tensor_tensor(
+                    z_bf[:, cols, :],
+                    acc[:, :, cols].rearrange("p t n -> p n t"),
+                    gs_t[:].unsqueeze(1).to_broadcast([P, HALF // 2, PACK]),
+                    ALU.mult,
+                )
+            for cols in pieces:
+                nc.vector.quantize_mx(
+                    out=codes[:, cols].bitcast(FP8X4), scales=scales[:, cols], in_=z_bf[:, cols, :].rearrange("p n t -> p (n t)")
+                )
             return codes, scales
 
         def pick_dictionary(u, tag):
@@ -168,7 +175,7 @@ def tile_picked_dhqierl_none_p_kernel(
             return got
 
         def second_product(b, ts, got, z):
-            bank = psum.tile([P, len(ts), HALF], F32, name="h_ps%d%d" % (b, ts[0]))
+            bank = psum.tile([P, len(ts), HALF], F32, name="h_ps%d%d" % (b, ts[0]), tag="bank_b" if (b, ts[0]) == (0, 0) else "h_ps%d%d" % (b, ts[0]))
             for v, t in enumerate(ts):
                 c0 = 2 * HALF + t * P
                 nc.tensor.matmul_mx(
@@ -188,27 +195,31 @@ def tile_picked_dhqierl_none_p_kernel(
                     nc.vector.tensor_scalar(h_part, bank[:, v, :], 0.0625, None, ALU.mult)
                 nc.scalar.activation(out=ds_sb[t][:].indirect(half_of(n1_t, b)), in_=h_part, func=ACT.Copy)
 
-        z_bf0 = weigh(0, y_ps0, "slot_c")
-        dw_got0 = pick_dictionary(0, "slot_a")
-        z0 = quantise(0, z_bf0)
+        z0 = quantise(0, y_ps0, "slot_c")
+        dw_got0 = pick_dictionary(0, 0)
         second_product(0, [0], dw_got0, z0)
         second_product(0, [1], dw_got0, z0)
         dw_got1 = pick_dictionary(1, "slot_c")
         second_product(0, [2, 3], dw_got1, z0)
-        z1 = quantise(1, weigh(1, y_ps1, None))
+        y_ps1 = first_product(1, xw_got1, plane_b)
+        z1 = quantise(1, y_ps1, None)
         second_product(1, [0, 1], dw_got0, z1)
         second_product(1, [2, 3], dw_got1, z1)
+        bias_t = tile([P, PACK], F32, "bias_t", "z_bf1")
+        nc.vector.scalar_tensor_tensor(bias_t[:], sl_t[:], -1.0, th_t[:], ALU.mult, ALU.mult)
 
         for t in range(PACK):
             sg = tile([P, S], F32, "sg%d" % t)
-            for b in range(2):
+            res = tile([P, S], F32, "res%d" % t)
+            width = HALF if t == PACK - 1 else S
+            for c0 in range(0, S, width):
+                cols = slice(c0, c0 + width)
                 nc.scalar.activation(
-                    out=sg[:, b * HALF : (b + 1) * HALF],
-                    in_=ds_sb[t][:].indirect(half_of(n2_t, b)),
+                    out=sg[:, cols],
+                    in_=ds_sb[t][:].indirect(n2_t[:, c0 // COLS : (c0 + width) // COLS]),
                     func=ACT.Sigmoid,
                     scale=sl_t[:, t : t + 1],
                     bias=bias_t[:, t : t + 1],
                 )
-            res = tile([P, S], F32, "res%d" % t)
-            nc.vector.tensor_tensor(res[:], h_sb[t][:], sg[:], ALU.mult)
-            nc.sync.dma_start(out=out[t * P : (t + 1) * P, :], in_=res[:])
+                nc.vector.tensor_tensor(res[:, cols], h_sb[t][:, cols], sg[:, cols], ALU.mult)
+                nc.sync.dma_start(out=out[t * P : (t + 1) * P, cols], in_=res[:, cols])

@@ -64,50 +64,49 @@ def tile_picked_dhqierl_none_p_kernel(
         nc.vector.memset(ds_tab[:].bitcast(I32), 0)
         w1s_raw = tile([P, H], U8, "w1s_raw")
         w2s_raw = tile([P, H], U8, "w2s_raw")
+        gs_t = tile([P, PACK], F32, "gs_t")
         offs_t = load_list(offs, "offs_t")
         load_repeated(nc.scalar, w1s_raw[:], w1_scales)
         load_repeated(nc.sync, xs_tab[:], x_scales)
-        load_repeated(nc.scalar, w2s_raw[:], w2_scales)
+        nc.scalar.dma_start(out=gs_t[:], in_=gs.rearrange("(p t) o -> p (t o)", t=PACK))
         hz_t = load_list(hz, "hz_t")
-        xw_tab = load_words(nc.scalar, x_words, "xw_tab")
-        k1_t = load_list(k1, "k1_t")
+        load_repeated(nc.scalar, w2s_raw[:], w2_scales)
+        xw_tab = load_words(nc.sync, x_words, "xw_tab")
         w1_raw = load_words(nc.scalar, w1_words, "w1_raw")
         warm_in = tile([P, 1], F32, "warm_in")
         nc.vector.memset(warm_in[:], 0.0)
         warm_out = tile([P, 1], F32, "warm_out")
         nc.scalar.activation(out=warm_out[:], in_=warm_in[:], func=ACT.Sigmoid)
-
-
         w2_raw = load_words(nc.sync, w2_words, "w2_raw")
+        k1_t = load_list(k1, "k1_t")
         load_scales(nc.sync, ds_tab[0:P:8, :], d_scales)
         n1_t = load_list(n1, "n1_t")
         n2_t = load_list(n2, "n2_t")
-        gs_t = tile([P, PACK], F32, "gs_t")
-        nc.gpsimd.dma_start(out=gs_t[:], in_=gs.rearrange("(p t) o -> p (t o)", t=PACK))
 
         x_lists = (offs_t, hz_t)
 
         plane_a = tile([P, 2 * HALF + 2 * H], U8, "plane_a")
-        for a, raw in enumerate((w1s_raw, w2s_raw)):
+
+        def deal_scales(a, raw):
             nc.vector.tensor_copy(
                 out=plane_a[:, 2 * HALF + a * H : 2 * HALF + (a + 1) * H].rearrange("p (t m) -> p t m", t=PACK),
                 in_=raw[:].rearrange("p (m t) -> p t m", t=PACK),
             )
-        got_a = tile([P, 2112], U8, "got_a", 0)
+
+        deal_scales(0, w1s_raw)
+        got_a = tile([P, 2240], U8, "got_a", 0)
         for a in range(2):
             nc.vector.tensor_copy(got_a[:, a * HALF : (a + 1) * HALF], xs_tab[:].indirect(half_of(x_lists[a], 0)))
+        deal_scales(1, w2s_raw)
         nc.vector.tensor_copy(out=plane_a[:, 0 : 2 * HALF].bitcast(I32), in_=got_a[:, 0 : 2 * HALF].bitcast(I32))
         place_rows(plane_a)
-        dw_tab = load_words(nc.sync, d_words, "dw_tab", 2048)
+        dw_tab = load_words(nc.sync, d_words, "dw_tab", 2176)
 
         w_dealt = []
         for a, raw in enumerate((w1_raw, w2_raw)):
             dealt = tile([P, H], U32, "w_dealt%d" % a)
             nc.scalar.copy(out=dealt[:].rearrange("p (t m) -> p m t", t=PACK), in_=raw[:].rearrange("p (m t) -> p m t", t=PACK))
             w_dealt.append(dealt)
-
-        sl_t = tile([P, PACK], F32, "sl_t", "w1_raw")
-        th_t = tile([P, PACK], F32, "th_t", "w2_raw")
 
         def pick_words(b, tag):
             got = tile([P, 2 * HALF], U32, "xw_got%d" % b, tag)
@@ -135,13 +134,15 @@ def tile_picked_dhqierl_none_p_kernel(
         y_ps0 = first_product(0, xw_got0, plane_a)
 
         plane_b = tile([P, 2 * HALF + H], U8, "plane_b")
-        got_b = tile([P, 2 * HALF + H], U8, "got_b", 1024)
+        got_b = tile([P, 1152], U8, "got_b", 1024)
         for a in range(2):
             nc.vector.tensor_copy(got_b[:, a * HALF : (a + 1) * HALF], xs_tab[:].indirect(half_of(x_lists[a], 1)))
-        nc.vector.tensor_copy(got_b[:, 2 * HALF :], ds_tab[:].indirect(k1_t[:]))
-        nc.vector.tensor_copy(out=plane_b[:].bitcast(I32), in_=got_b[:].bitcast(I32))
+        nc.vector.tensor_copy(got_b[:, 2 * HALF : 2 * HALF + H], ds_tab[:].indirect(k1_t[:]))
+        nc.vector.tensor_copy(out=plane_b[:].bitcast(I32), in_=got_b[:, 0 : 2 * HALF + H].bitcast(I32))
         place_rows(plane_b)
 
+        sl_t = tile([P, PACK], F32, "sl_t", 2048)
+        th_t = tile([P, PACK], F32, "th_t", 2112)
         with nc.allow_non_contiguous_dma(reason="one value a row, rows on the partitions"):
             nc.sync.dma_start(out=sl_t[:], in_=sl.rearrange("(t p) o -> p (t o)", p=P))
             nc.sync.dma_start(out=th_t[:], in_=th.rearrange("(t p) o -> p (t o)", p=P))
@@ -151,22 +152,17 @@ def tile_picked_dhqierl_none_p_kernel(
         h_sb = [tile([P, S], F32, "h_sb%d" % t) for t in range(PACK)]
         ds_sb = [tile([P, 2 * S], F32, "ds_sb%d" % t) for t in range(PACK)]
 
-        def quantise(b, acc, tag):
+        def weigh(b, acc, tag):
             z_bf = tile([P, HALF, PACK], BF16, "z_bf%d" % b, tag)
+            nc.vector.tensor_tensor(
+                z_bf[:], acc[:].rearrange("p t n -> p n t"), gs_t[:].unsqueeze(1).to_broadcast([P, HALF, PACK]), ALU.mult
+            )
+            return z_bf
+
+        def quantise(b, z_bf):
             codes = tile([P, HALF], U32, "z_codes%d" % b)
             scales = tile([P, HALF], U8, "z_scales%d" % b)
-            pieces = (slice(0, HALF // 2), slice(HALF // 2, HALF))
-            for cols in pieces:
-                nc.vector.tensor_tensor(
-                    z_bf[:, cols, :],
-                    acc[:, :, cols].rearrange("p t n -> p n t"),
-                    gs_t[:].unsqueeze(1).to_broadcast([P, HALF // 2, PACK]),
-                    ALU.mult,
-                )
-            for cols in pieces:
-                nc.vector.quantize_mx(
-                    out=codes[:, cols].bitcast(FP8X4), scales=scales[:, cols], in_=z_bf[:, cols, :].rearrange("p n t -> p (n t)")
-                )
+            nc.vector.quantize_mx(out=codes[:].bitcast(FP8X4), scales=scales[:], in_=z_bf[:].rearrange("p n t -> p (n t)"))
             return codes, scales
 
         def pick_dictionary(u, tag):
@@ -195,14 +191,15 @@ def tile_picked_dhqierl_none_p_kernel(
                     nc.vector.tensor_scalar(h_part, bank[:, v, :], 0.0625, None, ALU.mult)
                 nc.scalar.activation(out=ds_sb[t][:].indirect(half_of(n1_t, b)), in_=h_part, func=ACT.Copy)
 
-        z0 = quantise(0, y_ps0, "slot_c")
+        z_bf0 = weigh(0, y_ps0, "slot_c")
         dw_got0 = pick_dictionary(0, 0)
+        z0 = quantise(0, z_bf0)
         second_product(0, [0], dw_got0, z0)
         second_product(0, [1], dw_got0, z0)
         dw_got1 = pick_dictionary(1, "slot_c")
         second_product(0, [2, 3], dw_got1, z0)
         y_ps1 = first_product(1, xw_got1, plane_b)
-        z1 = quantise(1, y_ps1, None)
+        z1 = quantise(1, weigh(1, y_ps1, None))
         second_product(1, [0, 1], dw_got0, z1)
         second_product(1, [2, 3], dw_got1, z1)
         bias_t = tile([P, PACK], F32, "bias_t", "z_bf1")

from contextlib import ExitStack

import concourse.mybir as mybir

K, T, S, H, G = 512, 1024, 256, 512, 2048
FLOPS = 3 * 2 * K * H * S

F32 = mybir.dt.float32
BF16 = mybir.dt.bfloat16
I32 = mybir.dt.int32
U32 = mybir.dt.uint32
U16 = mybir.dt.uint16
U8 = mybir.dt.uint8
FP8X4 = mybir.dt.float8_e4m3fn_x4
ACT = mybir.ActivationFunctionType
ALU = mybir.AluOpType

P = 128
PACK = 4
HALF = 128
COLS = 16


def tile_picked_dhqierl_none_p_kernel(
    tc, x_words, x_scales, w1_words, w1_scales, w2_words, w2_scales, gs, d_words, d_scales, sl, th, offs, hz, k1, n1, n2, out
):
    nc = tc.nc
    with ExitStack() as ctx:
        keep = ctx.enter_context(tc.tile_pool(name="keep", bufs=1))
        stage = ctx.enter_context(tc.tile_pool(name="stage", bufs=1))
        psum = ctx.enter_context(tc.psum_pool(name="psum", bufs=1))

        def tile(shape, dtype, name, tag=None):
            if isinstance(tag, int):
                return stage.tile(shape, dtype, name=name, offset=tag, align_bytes=64)
            return keep.tile(shape, dtype, name=name, tag=tag or name, align_bytes=64)

        def load_list(src, name):
            dst = keep.tile([P, src.shape[1]], U16, name=name)
            nc.sync.dma_start(dst[:], src)
            return dst

        def load_words(queue, src, name, tag=None):
            dst = tile([P, src.shape[2]], U32, name, tag)
            queue.dma_start(out=dst[:].bitcast(I32), in_=src[0].rearrange("p n t -> p (n t)").bitcast(I32))
            return dst

        def load_scales(queue, dst, src):
            queue.dma_start(out=dst.bitcast(I32), in_=src[0].bitcast(I32))

        def load_repeated(queue, dst, src):
            rows = src[0].bitcast(I32)
            queue.dma_start(out=dst.bitcast(I32), in_=rows.unsqueeze(1).to_broadcast([16, 8, rows.shape[1]]))

        def place_rows(plane):
            for j in range(1, PACK):
                nc.sync.dma_start(out=plane[j:P:32, :].bitcast(I32), in_=plane[8 * j : P : 32, :].bitcast(I32))

        def half_of(lst, b):
            return lst[:, b * HALF // COLS : (b + 1) * HALF // COLS]

        xs_tab = tile([P, T], U8, "xs_tab")
        ds_tab = tile([P, G], U8, "ds_tab")
        nc.vector.memset(ds_tab[:].bitcast(I32), 0)
        w1s_raw = tile([P, H], U8, "w1s_raw")
        w2s_raw = tile([P, H], U8, "w2s_raw")
        gs_t = tile([P, PACK], F32, "gs_t")
        offs_t = load_list(offs, "offs_t")
        load_repeated(nc.scalar, w1s_raw[:], w1_scales)
        load_repeated(nc.sync, xs_tab[:], x_scales)
        nc.scalar.dma_start(out=gs_t[:], in_=gs.rearrange("(p t) o -> p (t o)", t=PACK))
        hz_t = load_list(hz, "hz_t")
        load_repeated(nc.scalar, w2s_raw[:], w2_scales)
        xw_tab = load_words(nc.sync, x_words, "xw_tab")
        w1_raw = load_words(nc.scalar, w1_words, "w1_raw")
        warm_in = tile([P, 1], F32, "warm_in")
        nc.vector.memset(warm_in[:], 0.0)
        warm_out = tile([P, 1], F32, "warm_out")
        nc.scalar.activation(out=warm_out[:], in_=warm_in[:], func=ACT.Sigmoid)
        w2_raw = load_words(nc.sync, w2_words, "w2_raw")
        k1_t = load_list(k1, "k1_t")
        load_scales(nc.sync, ds_tab[0:P:8, :], d_scales)
        n1_t = load_list(n1, "n1_t")
        n2_t = load_list(n2, "n2_t")

        x_lists = (offs_t, hz_t)

        plane_a = tile([P, 2 * HALF + 2 * H], U8, "plane_a")

        def deal_scales(a, raw):
            nc.vector.tensor_copy(
                out=plane_a[:, 2 * HALF + a * H : 2 * HALF + (a + 1) * H].rearrange("p (t m) -> p t m", t=PACK),
                in_=raw[:].rearrange("p (m t) -> p t m", t=PACK),
            )

        deal_scales(0, w1s_raw)
        got_a = tile([P, 2240], U8, "got_a", 0)
        for a in range(2):
            nc.vector.tensor_copy(got_a[:, a * HALF : (a + 1) * HALF], xs_tab[:].indirect(half_of(x_lists[a], 0)))
        deal_scales(1, w2s_raw)
        nc.vector.tensor_copy(out=plane_a[:, 0 : 2 * HALF].bitcast(I32), in_=got_a[:, 0 : 2 * HALF].bitcast(I32))
        place_rows(plane_a)
        dw_tab = load_words(nc.sync, d_words, "dw_tab", 2176)

        w_dealt = []
        for a, raw in enumerate((w1_raw, w2_raw)):
            dealt = tile([P, H], U32, "w_dealt%d" % a)
            nc.scalar.copy(out=dealt[:].rearrange("p (t m) -> p m t", t=PACK), in_=raw[:].rearrange("p (m t) -> p m t", t=PACK))
            w_dealt.append(dealt)

        def pick_words(b, tag):
            got = tile([P, 2 * HALF], U32, "xw_got%d" % b, tag)
            for a in range(2):
                nc.vector.tensor_copy(got[:, a * HALF : (a + 1) * HALF], xw_tab[:].indirect(half_of(x_lists[a], b)))
            return got

        def first_product(b, got, plane):
            acc = psum.tile([P, PACK, HALF], F32, name="y_ps%d" % b, tag=("bank_a", "bank_b")[b])
            for t in range(PACK):
                for a in range(2):
                    c0 = 2 * HALF + a * H + t * P
                    nc.tensor.matmul_mx(
                        out=acc[:, t, :],
                        lhsT=w_dealt[a][:, t * P : (t + 1) * P].bitcast(FP8X4),
                        lhsT_scale=plane_a[:, c0 : c0 + P],
                        rhs=got[:, a * HALF : (a + 1) * HALF].bitcast(FP8X4),
                        rhs_scale=plane[:, a * HALF : (a + 1) * HALF],
                        start=(a == 0),
                        stop=(a == 1),
                    )
            return acc

        xw_got0 = pick_words(0, 0)
        y_ps0 = first_product(0, xw_got0, plane_a)

        plane_b = tile([P, 2 * HALF + H], U8, "plane_b")
        got_b = tile([P, 1152], U8, "got_b", 1024)
        for a in range(2):
            nc.vector.tensor_copy(got_b[:, a * HALF : (a + 1) * HALF], xs_tab[:].indirect(half_of(x_lists[a], 1)))
        nc.vector.tensor_copy(got_b[:, 2 * HALF : 2 * HALF + H], ds_tab[:].indirect(k1_t[:]))
        nc.vector.tensor_copy(out=plane_b[:].bitcast(I32), in_=got_b[:, 0 : 2 * HALF + H].bitcast(I32))
        place_rows(plane_b)

        sl_t = tile([P, PACK], F32, "sl_t", 2048)
        th_t = tile([P, PACK], F32, "th_t", 2112)
        with nc.allow_non_contiguous_dma(reason="one value a row, rows on the partitions"):
            nc.sync.dma_start(out=sl_t[:], in_=sl.rearrange("(t p) o -> p (t o)", p=P))
            nc.sync.dma_start(out=th_t[:], in_=th.rearrange("(t p) o -> p (t o)", p=P))

        xw_got1 = pick_words(1, 1024)

        h_sb = [tile([P, S], F32, "h_sb%d" % t) for t in range(PACK)]
        ds_sb = [tile([P, 2 * S], F32, "ds_sb%d" % t) for t in range(PACK)]

        def weigh(b, acc, tag):
            z_bf = tile([P, HALF, PACK], BF16, "z_bf%d" % b, tag)
            nc.vector.tensor_tensor(
                z_bf[:], acc[:].rearrange("p t n -> p n t"), gs_t[:].unsqueeze(1).to_broadcast([P, HALF, PACK]), ALU.mult
            )
            return z_bf

        def quantise(b, z_bf):
            codes = tile([P, HALF], U32, "z_codes%d" % b)
            scales = tile([P, HALF], U8, "z_scales%d" % b)
            nc.vector.quantize_mx(out=codes[:].bitcast(FP8X4), scales=scales[:], in_=z_bf[:].rearrange("p n t -> p (n t)"))
            return codes, scales

        def pick_dictionary(u, tag):
            got = tile([P, 2 * P], U32, "dw_got%d" % u, tag)
            nc.vector.tensor_copy(got[:], dw_tab[:].indirect(k1_t[:, 16 * u : 16 * (u + 1)]))
            return got

        def second_product(b, ts, got, z):
            bank = psum.tile([P, len(ts), HALF], F32, name="h_ps%d%d" % (b, ts[0]), tag="bank_b" if (b, ts[0]) == (0, 0) else "h_ps%d%d" % (b, ts[0]))
            for v, t in enumerate(ts):
                c0 = 2 * HALF + t * P
                nc.tensor.matmul_mx(
                    out=bank[:, v, :],
                    lhsT=got[:, (t % 2) * P : (t % 2 + 1) * P].bitcast(FP8X4),
                    lhsT_scale=plane_b[:, c0 : c0 + P],
                    rhs=z[0][:].bitcast(FP8X4),
                    rhs_scale=z[1][:],
                    start=True,
                    stop=True,
                )
            for v, t in enumerate(ts):
                h_part = h_sb[t][:, b * HALF : (b + 1) * HALF]
                if b == 0 and t == 0:
                    nc.scalar.activation(out=h_part, in_=bank[:, v, :], func=ACT.Copy, scale=0.0625)
                else:
                    nc.vector.tensor_scalar(h_part, bank[:, v, :], 0.0625, None, ALU.mult)
                nc.scalar.activation(out=ds_sb[t][:].indirect(half_of(n1_t, b)), in_=h_part, func=ACT.Copy)

        z_bf0 = weigh(0, y_ps0, "slot_c")
        dw_got0 = pick_dictionary(0, 0)
        z0 = quantise(0, z_bf0)
        second_product(0, [0], dw_got0, z0)
        second_product(0, [1], dw_got0, z0)
        dw_got1 = pick_dictionary(1, "slot_c")
        second_product(0, [2, 3], dw_got1, z0)
        y_ps1 = first_product(1, xw_got1, plane_b)
        z1 = quantise(1, weigh(1, y_ps1, None))
        second_product(1, [0, 1], dw_got0, z1)
        second_product(1, [2, 3], dw_got1, z1)
        bias_t = tile([P, PACK], F32, "bias_t", "z_bf1")
        nc.vector.scalar_tensor_tensor(bias_t[:], sl_t[:], -1.0, th_t[:], ALU.mult, ALU.mult)

        for t in range(PACK):
            sg = tile([P, S], F32, "sg%d" % t)
            res = tile([P, S], F32, "res%d" % t)
            width = HALF if t == PACK - 1 else S
            for c0 in range(0, S, width):
                cols = slice(c0, c0 + width)
                nc.scalar.activation(
                    out=sg[:, cols],
                    in_=ds_sb[t][:].indirect(n2_t[:, c0 // COLS : (c0 + width) // COLS]),
                    func=ACT.Sigmoid,
                    scale=sl_t[:, t : t + 1],
                    bias=bias_t[:, t : t + 1],
                )
                nc.vector.tensor_tensor(res[:, cols], h_sb[t][:, cols], sg[:, cols], ALU.mult)
                nc.sync.dma_start(out=out[t * P : (t + 1) * P, cols], in_=res[:, cols])
